import numpy as np
CORES = [10,34,74,98]
N = 4
T, FF, CAPT = 2048, 32, 2048
def entries(a): return a.T.reshape(-1)
def pack(v, P): return np.ascontiguousarray(np.asarray(v, np.int32).reshape(-1, P).T)
def lists(rng, how):
    w = rng.random(N) ** 2 + 1e-3; c = T // 8 + ((CAPT - N * (T // 8)) * w / w.sum()).astype(np.int64)
    a = rng.permutation(N)
    if how == "few": c = np.zeros(N, np.int64); c[N - 1] = 3; c[int(rng.integers(N - 1))] = 1
    if how == "lone": s = int(rng.integers(CAPT - T + 1)); c = np.zeros(N, np.int64); c[a[0]] = T; c[a[1]] = s; c[a[2]] = CAPT - T - s
    if how == "none": c = np.zeros(N, np.int64)
    if how == "pair": s = 2 * int(rng.integers(512, 767)) + 1; c = np.zeros(N, np.int64); c[a[0]] = s; c[a[1]] = CAPT - s - 1; c[a[2]] = 1
    if how == "zeros": c = np.full(N, 2); c[0] = T - 7 - 2 * int(rng.integers(T // 16))
    K = np.stack([rng.permutation(np.arange(T) < c[r]) for r in range(N)])
    if how == "zeros": K = np.stack([np.r_[True, rng.permutation(np.arange(T - 2) < c[r] - 2), True] for r in range(N)])
    return {"keep": np.stack([pack(k, 16) for k in K])}
def blank(d):
    for r in range(N):
        k = entries(d["keep"][r]); d["x"][r][:, np.nonzero(k)[0][1:-1:4]] = 0; d["x"][r][:, np.nonzero(1 - k)[0][::4]] = 0
def setup_inputs(rng):
    return dict({"x": rng.standard_normal((N, 128, T), dtype=np.float32), "w1": np.repeat((rng.standard_normal((1, 128, FF * 128), dtype=np.float32) / 8), N, axis=0), "w2": np.repeat((rng.standard_normal((1, 128, FF * 128), dtype=np.float32) / 64), N, axis=0)}, **lists(rng, "uniform"))
def setup_inputs_few(rng):
    d = setup_inputs(rng); d.update(lists(rng, "few"))
    for k in ("x",): d[k] = (d[k].astype(np.float32) * 1024.0).astype(d[k].dtype)
    return d
def setup_inputs_lone(rng):
    d = setup_inputs(rng); d.update(lists(rng, "lone"))
    for k in ("x",): d[k] = (d[k].astype(np.float32) * (1 / 1024.0)).astype(d[k].dtype)
    return d
def setup_inputs_none(rng):
    d = setup_inputs(rng); d.update(lists(rng, "none"))
    return d
def setup_inputs_pair(rng):
    d = setup_inputs(rng); d.update(lists(rng, "pair"))
    return d
def setup_inputs_zeros(rng):
    d = setup_inputs(rng); d.update(lists(rng, "zeros"))
    blank(d)
    return d
def check_inputs(x):
    bad = []
    if x["keep"].min() < 0 or x["keep"].max() >= 2: bad.append("keep out of range")
    if int(x["keep"].sum()) > CAPT: bad.append("more than CAPT tokens are kept in all")
    if any((x[k] != x[k][:1]).any() for k in ("w1", "w2")): bad.append("w1 or w2 is not alike on all ranks")
    return bad
def reference(x, w1, w2, keep):
    X, W1, W2 = x.astype(np.float64), w1.astype(np.float64), w2.astype(np.float64)
    Y = X.copy()
    for r in range(N):
        P = np.nonzero(entries(keep[r]) == 1)[0]
        if len(P) == 0: continue
        Y[r][:, P] = sum(W2[r][:, 128 * f:128 * f + 128].T @ np.maximum(W1[r][:, 128 * f:128 * f + 128].T @ X[r][:, P], 0.0) for f in range(FF))
    return {"y": Y.astype(np.float32)}

@@ -1,0 +1,413 @@
+from concourse.bass import DstId, RemoteDMATransfer
+from concourse.mybir import AluOpType, ActivationFunctionType
+
+N = 4
+CORES_SIM = 112
+TOK = 2048
+CS = 512
+BL = 128
+ZC = 4
+XW = ZC + TOK
+WIN = 3 * TOK
+
+SCRATCH = {
+    "k2": ("sbuf", [128, 16], "int32"),
+    "s16": ("sbuf", [128, 256], "float32"),
+    "off": ("sbuf", [128, 16], "uint16"),
+    "cnt": ("sbuf", [128, 4], "float32"),
+    "ki": ("sbuf", [128, 8], "int32"),
+    "kc": ("sbuf", [128, 16], "float32"),
+    "im": ("sbuf", [128, 128], "float32"),
+    "tri": ("sbuf", [128, 128], "float32"),
+    "ones": ("sbuf", [128, 128], "float32"),
+    "ee": ("sbuf", [128, 144], "bfloat16"),
+    "ia": ("sbuf", [128, 256], "float32"),
+    "ib": ("sbuf", [128, 256], "float32"),
+    "va": ("sbuf", [128, 256], "float32"),
+    "vb": ("sbuf", [128, 256], "float32"),
+    "vv": ("sbuf", [128, 256], "bfloat16"),
+    "ww": ("sbuf", [128, WIN], "bfloat16"),
+    "lst": ("sbuf", [128, 128], "uint16"),
+    "i16": ("sbuf", [128, 128], "float32"),
+    "r16": ("sbuf", [128, 128], "float32"),
+    "i8": ("sbuf", [128, 8], "float32"),
+    "gm": ("sbuf", [128, 8], "float32"),
+    "fr": ("sbuf", [128, 128], "float32"),
+    "fo": ("sbuf", [128, 128], "uint16"),
+    "xg": ("sbuf", [128, XW + TOK], "float32"),
+    "sb": ("sbuf", [128, TOK], "float32"),
+    "rl": ("sbuf", [128, 768], "float32"),
+    "lnd": ("sbuf", [128, N * BL], "float32"),
+    "ta": ("sbuf", [128, BL], "float32"),
+    "tb": ("sbuf", [128, BL], "float32"),
+    "xc": ("sbuf", [128, CS], "float32"),
+    "w1s": ("sbuf", [128, 4096], "float32"),
+    "w2s": ("sbuf", [128, 4096], "float32"),
+    "hh": ("sbuf", [128, 2048], "float32"),
+    "yp": ("sbuf", [128, CS], "float32"),
+    "red": ("sbuf", [128, 8 * BL], "float32"),
+    "t4": ("sbuf", [128, 4 * BL], "float32"),
+    "t2": ("sbuf", [128, 2 * BL], "float32"),
+    "sm": ("sbuf", [128, BL], "float32"),
+    "yo": ("sbuf", [128, TOK], "float32"),
+    "hb0": ("psum", [128, 512], "float32"),
+    "hb1": ("psum", [128, 512], "float32"),
+    "hb2": ("psum", [128, 512], "float32"),
+    "hb3": ("psum", [128, 512], "float32"),
+    "yb0": ("psum", [128, 512], "float32"),
+    "yb1": ("psum", [128, 512], "float32"),
+    "pp": ("psum", [128, 512], "float32"),
+}
+SEMAPHORES = (["q_keep", "q_x", "q_w1a", "q_w1b", "q_w2a", "q_w2b", "q_y",
+               "gc1", "gc2", "gc3", "e_k", "vs", "e_z", "e_s", "e_p", "e_w", "e_l", "e_lst", "e_fr", "e_fp", "e_fo",
+               "e_own", "e_x", "e_ev0", "e_ev1", "e_so", "e_red", "e_y0", "e_y1",
+               "cnt_in", "fw", "w1_in", "w2_in", "xc0", "xc1", "rd", "gg", "ls"]
+              + ["gv%d" % i for i in range(4)] + ["ga%d" % i for i in range(4)] + ["rl_in%d" % i for i in range(3)]
+              + ["ha%d" % i for i in range(8)] + ["hr%d" % i for i in range(8)] + ["fin%d" % i for i in range(4)])
+
+ADD, SUB, MUL, MAX = AluOpType.add, AluOpType.subtract, AluOpType.mult, AluOpType.max
+COPY, RELU = ActivationFunctionType.Copy, ActivationFunctionType.Relu
+
+
+def bits(m):
+    return [1 << i for i in range(16) if m >> i & 1]
+
+
+def plan(T, topo, s):
+    R = T.cores[s]
+    ws = [R] + [c for c in range(CORES_SIM) if topo.chip(c) == topo.chip(R) and c != R]
+    ports = [c for c in ws if all(topo.may_write(c, d) for d in T.cores if d != c)]
+    near = [c for c in ports if topo.die(c) == topo.die(R)]
+    far = [c for c in ports if topo.die(c) != topo.die(R)]
+    return ws, [R, near[1], far[0], far[1]]
+
+
+POS = [0, 2, 1, 3]
+
+
+def rank_program(g, core, T, topo):
+    chip_of = [s for s in range(N) if topo.chip(T.cores[s]) == topo.chip(core)]
+    if not chip_of:
+        return
+    s = chip_of[0]
+    ws, owners = plan(T, topo, s)
+    R = ws[0]
+    me = ws.index(core)
+    is_r = core == R
+    own = owners.index(core) if core in owners else None
+    owner_at = [owners[POS.index(p)] for p in range(4)]
+    order = [(s + i) % N for i in range(1, N)]
+    V, A, E, Y, sem = g.vector, g.scalar, g.tensor, g.sync, T.sem
+    full = bits(topo.mask(core, ws[1] if is_r else R))
+    low = bits(topo.mask(core, T.cores[order[0]]))
+    up = [b for b in full if b not in low]
+    nls = [0]
+    nvs = [0]
+
+    def dst(c):
+        rid, pid, _ = topo.addr(c)
+        return DstId(rid=rid, pnc=pid)
+
+    def tr(src, out, to, rsem, eng):
+        nls[0] += len(eng)
+        return RemoteDMATransfer(dst_ids=[dst(c) for c in to], dma_engine_mask=sum(eng), remote_sem=rsem,
+                                 srcs=[src], dsts=[out for _ in to], alu_op=0)
+
+    def send(trs):
+        g.remote_dma_fused(trs, local_sem=sem.ls)
+
+    def v(ins):
+        ins.then_inc(sem.vs, 1)
+        nvs[0] += 1
+
+    def vw():
+        if nvs[0]:
+            V.wait_ge(sem.vs, nvs[0])
+
+    def cnt_masks(r):
+        n = N - 1 - r
+        return {1: [(0, 8)], 2: [(0, 4), (4, 8)], 3: [(0, 2), (2, 4), (4, 8)]}.get(n, [])
+
+    if is_r:
+        rank = s
+        kk, krow, kg, k16, grp = [T.ki[:, i:i + 1] for i in range(5)]
+        kcol, krowf, kgf, ma, mb, m2, c2, mc, jc = [T.kc[:, i:i + 1] for i in range(9)]
+        kf, sc, dd, d1, at_, ab, av, z16, jj, j4, f0, f1, f2, f3 = [T.s16[:, 16 * i:16 * i + 16] for i in range(14)]
+        last = T.s16[:, 31:32]
+        Y.dma_start(T.k2[:], T.keep[:]).then_inc(sem.q_keep, 16)
+        A.dma_start(T.xg[:, ZC:XW], T.x[:]).then_inc(sem.q_x, 16)
+        Y.dma_start(T.w1s[:, 0:2048], T.w1[:, 0:2048]).then_inc(sem.q_w1a, 16)
+        Y.wait_ge(sem.q_x, 16)
+        Y.dma_start(T.w1s[:, 2048:4096], T.w1[:, 2048:4096]).then_inc(sem.q_w1b, 16)
+        Y.wait_ge(sem.q_w1a, 16)
+        Y.dma_start(T.w2s[:, 0:2048], T.w2[:, 0:2048]).then_inc(sem.q_w2a, 16)
+        Y.wait_ge(sem.q_w1b, 16)
+        Y.dma_start(T.w2s[:, 2048:4096], T.w2[:, 2048:4096]).then_inc(sem.q_w2b, 16)
+
+        ok = {"allow_small_or_imprecise_dtypes": True}
+        g.iota(kk, [[0, 1]], 0, 1).then_inc(sem.gc1, 1)
+        g.iota(T.im[:], [[1, 128]], 0, 0, **ok).then_inc(sem.gc1, 1)
+        g.iota(dd, [[1, 16]], TOK, 16, **ok).then_inc(sem.gc1, 1)
+
+        V.memset(T.xg[:, 0:ZC], 0.0).then_inc(sem.e_z, 1)
+        v(V.memset(z16, 0.0))
+        v(V.memset(T.ee[:], 0.0))
+        V.memset(T.ones[:], 1.0).then_inc(sem.e_k, 1)
+        vw()
+        V.memset(T.ee[:, 0:144:16], 1.0).then_inc(sem.e_k, 1)
+        V.wait_ge(sem.gc1, 3)
+        v(V.tensor_copy(kcol, kk))
+        v(V.tensor_scalar(d1, dd, 1.0, None, ADD))
+        v(V.memset(T.ww[:, 0:TOK], 0.0))
+        vw()
+        V.tensor_scalar(T.tri[:], T.im[:], kcol, None, AluOpType.is_gt).then_inc(sem.e_k, 1)
+
+        V.wait_ge(sem.q_keep, 16)
+        v(V.tensor_copy(kf, T.k2[:]))
+        vw()
+        V.tensor_tensor_scan(sc, kf, z16, 0.0, ADD, ADD).then_inc(sem.e_s, 1)
+
+        g.wait_ge(sem.e_s, 1)
+        later = list(range(rank + 1, N))
+        if later:
+            send([tr(last, T.cnt[:, rank:rank + 1], [T.cores[d]], sem.cnt_in, low[a:b])
+                  for d, (a, b) in zip(later, cnt_masks(rank))])
+        g.iota(T.ia[:], [[0, 16], [0, 2], [256, 8]], 0, 0, **ok).then_inc(sem.gc2, 1)
+        g.iota(T.ib[:], [[16, 16], [1, 2], [0, 8]], 0, 0, **ok).then_inc(sem.gc2, 1)
+        g.iota(T.i16[:], [[0, 8], [1, 16]], 0, 0, **ok).then_inc(sem.gc3, 1)
+        g.iota(T.i8[:], [[1, 8]], 0, 0, **ok).then_inc(sem.gc3, 1)
+        g.iota(jj, [[16, 16]], ZC, 0, **ok).then_inc(sem.gc3, 1)
+
+        E.wait_ge(sem.e_k, 3)
+        E.wait_ge(sem.e_s, 1)
+        mm = E.matmul(T.pp[:, 0:1], T.tri[:], last, True, rank == 0)
+        if rank:
+            E.wait_ge(sem.cnt_in, sum(b - a for r in range(rank) for a, b in [cnt_masks(r)[rank - r - 1]]))
+            for r in range(rank):
+                mm = E.matmul(T.pp[:, 0:1], T.ones[:], T.cnt[:, r:r + 1], False, r == rank - 1)
+        mm.then_inc(sem.e_p, 1)
+
+        V.wait_ge(sem.e_s, 1)
+        v(V.tensor_tensor(at_, sc, d1, SUB))
+        shr, band, eq = AluOpType.arith_shift_right, AluOpType.bitwise_and, AluOpType.is_equal
+        v(V.tensor_scalar(krow, kk, 3, None, shr))
+        v(V.tensor_scalar(kg, kk, 7, None, band))
+        v(V.tensor_scalar(k16, kk, 15, None, band))
+        v(V.tensor_scalar(grp, kk, 4, None, shr))
+        vw()
+        v(V.tensor_tensor(ab, at_, kf, MUL))
+        v(V.tensor_copy(krowf, krow))
+        v(V.tensor_copy(kgf, kg))
+        v(V.tensor_scalar(ma, k16, 0.0, None, eq))
+        v(V.tensor_scalar(mb, k16, 1.0, None, eq))
+        v(V.tensor_scalar(m2, k16, 2.0, None, eq))
+        v(V.tensor_scalar(c2, grp, 2.0, 4.0, MUL, ADD))
+        vw()
+        v(V.tensor_tensor(av, ab, dd, ADD))
+        v(V.tensor_tensor(mc, m2, c2, MUL))
+        v(V.tensor_scalar(jc, kgf, 256.0, krowf, MUL, ADD))
+        V.wait_ge(sem.gc2, 2)
+        v(V.tensor_scalar(T.va[:], T.ia[:], ma, None, MUL))
+        vw()
+        v(V.tensor_scalar(T.vb[:], T.ib[:], mb, mc, MUL, ADD))
+        vw()
+        v(V.tensor_tensor(T.vv[:], T.va[:], T.vb[:], ADD))
+        V.wait_ge(sem.e_p, 1)
+        v(V.tensor_scalar(T.off[:], av, T.pp[:, 0:1], None, ADD))
+        vw()
+        V.tensor_copy(T.ww[:, 0:WIN].indirect(T.off[:, 0:16]), T.vv[:]).then_inc(sem.e_w, 1)
+
+        E.wait_ge(sem.e_w, 1)
+        for a in range(16):
+            mm = E.matmul(T.hb0[:, 0:128], T.ee[:, 16 - a:144 - a], T.ww[:, a:TOK:16], a == 0, a == 15)
+        mm.then_inc(sem.e_l, 1)
+        V.wait_ge(sem.e_l, 1)
+        V.tensor_copy(T.lst[:], T.hb0[:, 0:128]).then_inc(sem.e_lst, 1)
+
+        for q in (V, A):
+            q.wait_ge(sem.q_x, 16)
+            q.wait_ge(sem.e_z, 1)
+            q.wait_ge(sem.e_lst, 1)
+        xw = T.xg[:, 0:XW]
+        for i, d in enumerate(order + [s]):
+            c, l = CS * d, 32 * d
+            V.tensor_copy(T.sb[:, c + 256:c + 512], xw.indirect(T.lst[:, l + 16:l + 32])).then_inc(sem["gv%d" % i], 1)
+            if d != s:
+                A.activation(T.sb[:, c:c + 256], xw.indirect(T.lst[:, l:l + 16]), COPY).then_inc(sem["ga%d" % i], 1)
+            else:
+                A.activation(T.sb[:, c + 128:c + 256], xw.indirect(T.lst[:, l + 8:l + 16]), COPY).then_inc(sem["ga%d" % i], 1)
+                A.activation(T.lnd[:, s * BL:s * BL + BL], xw.indirect(T.lst[:, l:l + 8]), COPY).then_inc(sem.e_own, 1)
+
+        g.wait_ge(sem.q_w1a, 16)
+        send([tr(T.w1s[:, CS * k:CS * k + CS], T.w1s[:, 0:CS], [ws[k]], sem.w1_in, full[4 * k - 4:4 * k]) for k in (1, 2, 3)])
+        for i, d in enumerate(order):
+            c = CS * d
+            _, od = plan(T, topo, d)
+            g.wait_ge(sem["gv%d" % i], 1)
+            send([tr(T.sb[:, c + 256:c + 512], T.rl[:, 256 * i:256 * i + 256], [owners[2]], sem["rl_in%d" % i], up)])
+            g.wait_ge(sem["ga%d" % i], 1)
+            send([tr(T.sb[:, c + BL * o:c + BL * o + BL], T.lnd[:, s * BL:s * BL + BL], [od[o]], sem.fw, low[4 * o:4 * o + 4])
+                  for o in (0, 1)])
+        g.wait_ge(sem.gv3, 1)
+        g.wait_ge(sem.ga3, 1)
+        c = CS * s
+        send([tr(T.sb[:, c + BL * o:c + BL * o + BL], T.lnd[:, s * BL:s * BL + BL], [owners[o]], sem.fw, full[4 * o:4 * o + 4])
+              for o in (1, 2, 3)])
+        g.wait_ge(sem.q_w1b, 16)
+        send([tr(T.w1s[:, CS * k:CS * k + CS], T.w1s[:, 0:CS], [ws[k]], sem.w1_in, up[2 * k - 8:2 * k - 6]) for k in (4, 5, 6, 7)])
+        g.wait_ge(sem.q_w2a, 16)
+        send([tr(T.w2s[:, CS * k:CS * k + CS], T.w2s[:, 0:CS], [ws[k]], sem.w2_in, up[2 * k:2 * k + 2]) for k in (1, 2, 3)])
+        g.wait_ge(sem.q_w2b, 16)
+        send([tr(T.w2s[:, CS * k:CS * k + CS], T.w2s[:, 0:CS], [ws[k]], sem.w2_in, low[2 * k - 8:2 * k - 6]) for k in (4, 5, 6, 7)])
+
+        V.wait_ge(sem.gc3, 3)
+        v(V.tensor_scalar(T.r16[:], T.i16[:], krowf, None, eq))
+        v(V.tensor_scalar(T.gm[:], T.i8[:], kgf, None, eq))
+        v(V.tensor_scalar(j4, jj, jc, None, ADD))
+        v(V.tensor_scalar(f0, sc, T.pp[:, 0:1], float(XW - 1), ADD, ADD))
+        vw()
+        v(V.tensor_tensor(f1, f0, j4, SUB))
+        vw()
+        v(V.tensor_tensor(f2, f1, kf, MUL))
+        vw()
+        v(V.tensor_tensor(f3, f2, j4, ADD))
+        vw()
+        for i in range(8):
+            V.tensor_scalar(T.fr[:, 16 * i:16 * i + 16], f3, T.gm[:, i:i + 1], None, MUL).then_inc(sem.e_fr, 1)
+        E.wait_ge(sem.e_fr, 8)
+        E.matmul(T.hb1[:, 0:128], T.r16[:], T.fr[:], True, True).then_inc(sem.e_fp, 1)
+        V.wait_ge(sem.e_fp, 1)
+        V.tensor_copy(T.fo[:], T.hb1[:, 0:128]).then_inc(sem.e_fo, 1)
+        E.wait_ge(sem.e_lst, 1)
+        E.wait_ge(sem.e_fo, 1)
+
+    if own == 2:
+        for i, d in enumerate(order):
+            _, od = plan(T, topo, d)
+            g.wait_ge(sem["rl_in%d" % i], 8)
+            send([tr(T.rl[:, 256 * i + BL * o:256 * i + BL * o + BL], T.lnd[:, s * BL:s * BL + BL], [od[2 + o]], sem.fw,
+                     low[4 * o:4 * o + 4]) for o in (0, 1)])
+
+    if own is not None:
+        p = POS[own]
+        V.wait_ge(sem.fw, 12 if is_r else 16)
+        if is_r:
+            V.wait_ge(sem.e_own, 1)
+        v(V.tensor_tensor(T.ta[:], T.lnd[:, 0:BL], T.lnd[:, BL:2 * BL], ADD))
+        v(V.tensor_tensor(T.tb[:], T.lnd[:, 2 * BL:3 * BL], T.lnd[:, 3 * BL:4 * BL], ADD))
+        vw()
+        blk = T.xc[:, p * BL:p * BL + BL]
+        V.tensor_tensor(blk, T.ta[:], T.tb[:], ADD).then_inc(sem.e_x, 1)
+        g.wait_ge(sem.e_x, 1)
+        send([tr(blk, blk, [c for c in ws if c != core], sem["xc%d" % (p // 2)], full)])
+
+    hb = [T.hb0, T.hb1, T.hb2, T.hb3]
+    yb = [T.yb0, T.yb1]
+
+    def layer1(n):
+        h, i = n // 4, n % 4
+        if i == 0:
+            others = [c for c in owner_at[2 * h:2 * h + 2] if c != core]
+            E.wait_ge(sem["xc%d" % h], 16 * len(others))
+            if len(others) == 1:
+                E.wait_ge(sem.e_x, 1)
+        E.matmul(hb[n % 4][:, 0:256], T.w1s[:, 128 * i:128 * i + 128], T.xc[:, 256 * h:256 * h + 256], True, True).then_inc(sem["ha%d" % n], 1)
+        hs = T.hh[:, 256 * n:256 * n + 256]
+        if n % 2 == 0:
+            A.wait_ge(sem["ha%d" % n], 1)
+            A.activation(hs, hb[n % 4][:, 0:256], RELU).then_inc(sem["hr%d" % n], 1)
+        else:
+            V.wait_ge(sem["ha%d" % n], 1)
+            V.tensor_scalar(hs, hb[n % 4][:, 0:256], 0.0, None, MAX).then_inc(sem["hr%d" % n], 1)
+
+    def layer2(n):
+        h, i = n // 4, n % 4
+        E.wait_ge(sem["hr%d" % n], 1)
+        m = E.matmul(yb[h][:, 0:256], T.w2s[:, 128 * i:128 * i + 128], T.hh[:, 256 * n:256 * n + 256], i == 0, i == 3)
+        if i == 3:
+            m.then_inc(sem["e_y%d" % h], 1)
+
+    def home(h):
+        q = A if h else V
+        q.wait_ge(sem["e_y%d" % h], 1)
+
+        def copy(out, in_):
+            return A.activation(out, in_, COPY) if h else V.tensor_copy(out, in_)
+        pair = owner_at[2 * h:2 * h + 2]
+        c = 256 * h
+        if core in pair:
+            b = pair.index(core)
+            o = 1 - b
+            copy(T.yp[:, c + BL * o:c + BL * o + BL], yb[h][:, BL * o:BL * o + BL]).then_inc(sem["e_ev%d" % h], 1)
+            copy(T.red[:, me * BL:me * BL + BL], yb[h][:, BL * b:BL * b + BL]).then_inc(sem.e_so, 1)
+            todo = [(o, full)]
+        else:
+            copy(T.yp[:, c:c + 256], yb[h][:, 0:256]).then_inc(sem["e_ev%d" % h], 1)
+            todo = [(0, full[0:8]), (1, full[8:16])]
+        g.wait_ge(sem["e_ev%d" % h], 1)
+        send([tr(T.yp[:, c + BL * o:c + BL * o + BL], T.red[:, me * BL:me * BL + BL], [pair[o]], sem.rd, e) for o, e in todo])
+
+    def collect():
+        V.wait_ge(sem.rd, 6 * 8 + 16)
+        V.wait_ge(sem.e_so, 1)
+        v(V.tensor_tensor(T.t4[:], T.red[:, 0:512], T.red[:, 512:1024], ADD))
+        vw()
+        v(V.tensor_tensor(T.t2[:], T.t4[:, 0:256], T.t4[:, 256:512], ADD))
+        vw()
+        at = XW + CS * s + BL * own
+        out = T.xg[:, at:at + BL] if is_r else T.sm[:]
+        V.tensor_tensor(out, T.t2[:, 0:128], T.t2[:, 128:256], ADD).then_inc(sem.e_red, 1)
+
+    def deliver():
+        at = XW + CS * s + BL * own
+        slot = T.xg[:, at:at + BL]
+        out = slot if is_r else T.sm[:]
+        g.wait_ge(sem.e_red, 1)
+        trs = [tr(out, slot, [T.cores[d] for d in order], sem.gg, low)]
+        if not is_r:
+            trs.append(tr(out, slot, [R], sem.gg, up))
+        send(trs)
+
+    if not is_r:
+        E.wait_ge(sem.w1_in, 4 if me < 4 else 2)
+    else:
+        E.wait_ge(sem.q_w1a, 16)
+    layer1(0)
+    layer1(1)
+    if not is_r:
+        E.wait_ge(sem.w2_in, 2)
+    else:
+        E.wait_ge(sem.q_w2a, 16)
+    for n in range(8):
+        layer2(n)
+        if n + 2 < 8:
+            layer1(n + 2)
+        if n == 3:
+            home(0)
+    early = own is not None and POS[own] < 2
+    if early:
+        collect()
+    home(1)
+    if own is not None:
+        if not early:
+            collect()
+        deliver()
+
+    if is_r:
+        for q in (V, A):
+            q.wait_ge(sem.gg, 15 * 8)
+            q.wait_ge(sem.e_red, 1)
+            q.wait_ge(sem.e_fo, 1)
+        for c in (0, 2, 1, 3):
+            src = T.xg[:].indirect(T.fo[:, 32 * c:32 * c + 32])
+            out = T.yo[:, CS * c:CS * c + CS]
+            ins = V.tensor_copy(out, src) if c < 2 else A.activation(out, src, COPY)
+            ins.then_inc(sem["fin%d" % c], 1)
+        for c in (0, 2, 1, 3):
+            Y.wait_ge(sem["fin%d" % c], 1)
+            Y.dma_start(T.y[:, CS * c:CS * c + CS], T.yo[:, CS * c:CS * c + CS]).then_inc(sem.q_y, 16)
+        Y.wait_ge(sem.q_y, 64)
+
+    vw()
+    if nls[0]:
+        g.wait_ge(sem.ls, nls[0])

@@ -6,6 +6,7 @@ CORES_SIM = 112
 TOK = 2048
 CS = 512
 BL = 128
+HB = 64
 ZC = 4
 XW = ZC + TOK
 WIN = 3 * TOK
@@ -17,7 +18,6 @@ SCRATCH = {
     "cnt": ("sbuf", [128, 4], "float32"),
     "ki": ("sbuf", [128, 8], "int32"),
     "kc": ("sbuf", [128, 16], "float32"),
-    "im": ("sbuf", [128, 128], "float32"),
     "tri": ("sbuf", [128, 128], "float32"),
     "ones": ("sbuf", [128, 128], "float32"),
     "ee": ("sbuf", [128, 144], "bfloat16"),
@@ -36,7 +36,7 @@ SCRATCH = {
     "fo": ("sbuf", [128, 128], "uint16"),
     "xg": ("sbuf", [128, XW + TOK], "float32"),
     "sb": ("sbuf", [128, TOK], "float32"),
-    "rl": ("sbuf", [128, 768], "float32"),
+    "rl": ("sbuf", [128, 3 * BL], "float32"),
     "lnd": ("sbuf", [128, N * BL], "float32"),
     "ta": ("sbuf", [128, BL], "float32"),
     "tb": ("sbuf", [128, BL], "float32"),
@@ -45,10 +45,10 @@ SCRATCH = {
     "w2s": ("sbuf", [128, 4096], "float32"),
     "hh": ("sbuf", [128, 2048], "float32"),
     "yp": ("sbuf", [128, CS], "float32"),
-    "red": ("sbuf", [128, 8 * BL], "float32"),
-    "t4": ("sbuf", [128, 4 * BL], "float32"),
-    "t2": ("sbuf", [128, 2 * BL], "float32"),
-    "sm": ("sbuf", [128, BL], "float32"),
+    "red": ("sbuf", [128, 2 * 8 * HB], "float32"),
+    "t4": ("sbuf", [128, 2 * 4 * HB], "float32"),
+    "t2": ("sbuf", [128, 2 * 2 * HB], "float32"),
+    "sm": ("sbuf", [128, 2 * HB], "float32"),
     "yo": ("sbuf", [128, TOK], "float32"),
     "hb0": ("psum", [128, 512], "float32"),
     "hb1": ("psum", [128, 512], "float32"),
@@ -56,17 +56,18 @@ SCRATCH = {
     "hb3": ("psum", [128, 512], "float32"),
     "yb0": ("psum", [128, 512], "float32"),
     "yb1": ("psum", [128, 512], "float32"),
-    "pp": ("psum", [128, 512], "float32"),
+    "yb2": ("psum", [128, 512], "float32"),
+    "yb3": ("psum", [128, 512], "float32"),
 }
-SEMAPHORES = (["q_keep", "q_x", "q_w1a", "q_w1b", "q_w2a", "q_w2b", "q_y",
-               "gc1", "gc2", "gc3", "e_k", "vs", "e_z", "e_s", "e_p", "e_w", "e_l", "e_lst", "e_fr", "e_fp", "e_fo",
-               "e_own", "e_x", "e_ev0", "e_ev1", "e_so", "e_red", "e_y0", "e_y1",
-               "cnt_in", "fw", "w1_in", "w2_in", "xc0", "xc1", "rd", "gg", "ls"]
-              + ["gv%d" % i for i in range(4)] + ["ga%d" % i for i in range(4)] + ["rl_in%d" % i for i in range(3)]
-              + ["ha%d" % i for i in range(8)] + ["hr%d" % i for i in range(8)] + ["fin%d" % i for i in range(4)])
+SEMAPHORES = (["q_keep", "q_x", "q_w1a", "q_w1b", "q_w2a", "q_w2b", "q_y", "go",
+               "gc1", "gc2", "gc3", "gc4", "e_k", "e_o", "e_m", "e_va", "vs", "e_z", "e_s", "e_p", "e_w", "e_fr", "e_fp", "e_fo",
+               "e_x", "cnt_in", "w1_in", "w2_in", "gg", "ls", "lc"]
+              + ["%s%d" % (n, i) for n in ("gv", "ga", "fw", "rl_in", "xc", "e_y", "e_ev", "e_so") for i in range(4)]
+              + ["%s%d" % (n, i) for n in ("e_l", "e_lst", "rd", "e_red") for i in range(2)]
+              + ["%s%d" % (n, i) for n in ("ha", "hr") for i in range(8)] + ["fin%d" % i for i in range(6)])
 
 ADD, SUB, MUL, MAX = AluOpType.add, AluOpType.subtract, AluOpType.mult, AluOpType.max
-COPY, RELU = ActivationFunctionType.Copy, ActivationFunctionType.Relu
+COPY, RELU, IDENT = ActivationFunctionType.Copy, ActivationFunctionType.Relu, ActivationFunctionType.Identity
 
 
 def bits(m):
@@ -75,14 +76,14 @@ def bits(m):
 
 def plan(T, topo, s):
     R = T.cores[s]
-    ws = [R] + [c for c in range(CORES_SIM) if topo.chip(c) == topo.chip(R) and c != R]
-    ports = [c for c in ws if all(topo.may_write(c, d) for d in T.cores if d != c)]
-    near = [c for c in ports if topo.die(c) == topo.die(R)]
+    cs = [c for c in range(CORES_SIM) if topo.chip(c) == topo.chip(R)]
+    ports = [c for c in cs if all(topo.may_write(c, d) for d in T.cores if d != c)]
+    near = [c for c in ports if topo.die(c) == topo.die(R) and c != R]
     far = [c for c in ports if topo.die(c) != topo.die(R)]
-    return ws, [R, near[1], far[0], far[1]]
-
-
-POS = [0, 2, 1, 3]
+    rest = [c for c in cs if c not in ports]
+    adders = [c for c in rest if topo.die(c) == topo.die(R)] + [c for c in rest if topo.die(c) != topo.die(R)]
+    ws = [R, adders[0], near[0], adders[1], adders[2], far[0], adders[3], far[1]]
+    return ws, [R, near[0], far[0], far[1]], adders
 
 
 def rank_program(g, core, T, topo):
@@ -90,12 +91,10 @@ def rank_program(g, core, T, topo):
     if not chip_of:
         return
     s = chip_of[0]
-    ws, owners = plan(T, topo, s)
+    ws, ports, adders = plan(T, topo, s)
     R = ws[0]
     me = ws.index(core)
     is_r = core == R
-    own = owners.index(core) if core in owners else None
-    owner_at = [owners[POS.index(p)] for p in range(4)]
     order = [(s + i) % N for i in range(1, N)]
     V, A, E, Y, sem = g.vector, g.scalar, g.tensor, g.sync, T.sem
     full = bits(topo.mask(core, ws[1] if is_r else R))
@@ -131,140 +130,163 @@ def rank_program(g, core, T, topo):
     if is_r:
         rank = s
         kk, krow, kg, k16, grp = [T.ki[:, i:i + 1] for i in range(5)]
-        kcol, krowf, kgf, ma, mb, m2, c2, mc, jc = [T.kc[:, i:i + 1] for i in range(9)]
+        krowf, kgf, ma, mb, m2, c2, mc, jc = [T.kc[:, i:i + 1] for i in range(8)]
         kf, sc, dd, d1, at_, ab, av, z16, jj, j4, f0, f1, f2, f3 = [T.s16[:, 16 * i:16 * i + 16] for i in range(14)]
         last = T.s16[:, 31:32]
+        pp = T.yb3[:, 0:1]
+        shr, band, eq = AluOpType.arith_shift_right, AluOpType.bitwise_and, AluOpType.is_equal
+        later = list(range(rank + 1, N))
         Y.dma_start(T.k2[:], T.keep[:]).then_inc(sem.q_keep, 16)
-        A.dma_start(T.xg[:, ZC:XW], T.x[:]).then_inc(sem.q_x, 16)
+        Y.dma_start(T.xg[:, ZC:XW], T.x[:]).then_inc(sem.q_x, 16)
         Y.dma_start(T.w1s[:, 0:2048], T.w1[:, 0:2048]).then_inc(sem.q_w1a, 16)
-        Y.wait_ge(sem.q_x, 16)
+        if later:
+            Y.wait_ge(sem.lc, sum(b - a for a, b in cnt_masks(rank)))
+        else:
+            Y.wait_ge(sem.q_w1a, 16)
         Y.dma_start(T.w1s[:, 2048:4096], T.w1[:, 2048:4096]).then_inc(sem.q_w1b, 16)
-        Y.wait_ge(sem.q_w1a, 16)
-        Y.dma_start(T.w2s[:, 0:2048], T.w2[:, 0:2048]).then_inc(sem.q_w2a, 16)
         Y.wait_ge(sem.q_w1b, 16)
+        Y.dma_start(T.w2s[:, 0:2048], T.w2[:, 0:2048]).then_inc(sem.q_w2a, 16)
+        Y.wait_ge(sem.go, 1)
         Y.dma_start(T.w2s[:, 2048:4096], T.w2[:, 2048:4096]).then_inc(sem.q_w2b, 16)
 
         ok = {"allow_small_or_imprecise_dtypes": True}
         g.iota(kk, [[0, 1]], 0, 1).then_inc(sem.gc1, 1)
-        g.iota(T.im[:], [[1, 128]], 0, 0, **ok).then_inc(sem.gc1, 1)
-        g.iota(dd, [[1, 16]], TOK, 16, **ok).then_inc(sem.gc1, 1)
+        g.iota(T.ia[:], [[0, 16], [0, 2], [256, 8]], 0, 0, **ok).then_inc(sem.gc2, 1)
+        g.iota(T.ib[:], [[16, 16], [1, 2], [0, 8]], 0, 0, **ok).then_inc(sem.gc2, 1)
+        g.wait_ge(sem.e_o, 1)
+        g.affine_select(T.tri[:], T.ones[:], [[1, 128]], AluOpType.is_gt, 0.0, 0, -1).then_inc(sem.e_k, 1)
 
-        V.memset(T.xg[:, 0:ZC], 0.0).then_inc(sem.e_z, 1)
+        V.memset(T.ones[:], 1.0).then_inc(sem.e_o, 1)
         v(V.memset(z16, 0.0))
         v(V.memset(T.ee[:], 0.0))
-        V.memset(T.ones[:], 1.0).then_inc(sem.e_k, 1)
+        V.wait_ge(sem.gc1, 1)
+        v(V.tensor_scalar(k16, kk, 15, None, band))
+        v(V.tensor_scalar(grp, kk, 4, None, shr))
         vw()
         V.memset(T.ee[:, 0:144:16], 1.0).then_inc(sem.e_k, 1)
-        V.wait_ge(sem.gc1, 3)
-        v(V.tensor_copy(kcol, kk))
-        v(V.tensor_scalar(d1, dd, 1.0, None, ADD))
-        v(V.memset(T.ww[:, 0:TOK], 0.0))
+        v(V.tensor_scalar(m2, k16, 2.0, None, eq))
+        v(V.tensor_scalar(c2, grp, 2.0, 4.0, MUL, ADD))
+        V.tensor_scalar(ma, k16, 0.0, None, eq).then_inc(sem.e_m, 1)
+        V.tensor_scalar(mb, k16, 1.0, None, eq).then_inc(sem.e_m, 1)
         vw()
-        V.tensor_scalar(T.tri[:], T.im[:], kcol, None, AluOpType.is_gt).then_inc(sem.e_k, 1)
+        V.tensor_tensor(mc, m2, c2, MUL).then_inc(sem.e_m, 1)
 
         V.wait_ge(sem.q_keep, 16)
         v(V.tensor_copy(kf, T.k2[:]))
         vw()
         V.tensor_tensor_scan(sc, kf, z16, 0.0, ADD, ADD).then_inc(sem.e_s, 1)
 
-        g.wait_ge(sem.e_s, 1)
-        later = list(range(rank + 1, N))
         if later:
-            send([tr(last, T.cnt[:, rank:rank + 1], [T.cores[d]], sem.cnt_in, low[a:b])
-                  for d, (a, b) in zip(later, cnt_masks(rank))])
-        g.iota(T.ia[:], [[0, 16], [0, 2], [256, 8]], 0, 0, **ok).then_inc(sem.gc2, 1)
-        g.iota(T.ib[:], [[16, 16], [1, 2], [0, 8]], 0, 0, **ok).then_inc(sem.gc2, 1)
+            g.wait_ge(sem.e_s, 1)
+            g.remote_dma_fused([tr(last, T.cnt[:, rank:rank + 1], [T.cores[d]], sem.cnt_in, low[a:b])
+                                for d, (a, b) in zip(later, cnt_masks(rank))], local_sem=sem.lc)
+            nls[0] = 0
+        g.iota(dd, [[1, 16]], TOK, 16, **ok).then_inc(sem.gc4, 1)
         g.iota(T.i16[:], [[0, 8], [1, 16]], 0, 0, **ok).then_inc(sem.gc3, 1)
         g.iota(T.i8[:], [[1, 8]], 0, 0, **ok).then_inc(sem.gc3, 1)
         g.iota(jj, [[16, 16]], ZC, 0, **ok).then_inc(sem.gc3, 1)
 
-        E.wait_ge(sem.e_k, 3)
+        E.wait_ge(sem.e_k, 2)
+        E.wait_ge(sem.e_o, 1)
         E.wait_ge(sem.e_s, 1)
-        mm = E.matmul(T.pp[:, 0:1], T.tri[:], last, True, rank == 0)
+        mm = E.matmul(pp, T.tri[:], last, True, rank == 0)
         if rank:
             E.wait_ge(sem.cnt_in, sum(b - a for r in range(rank) for a, b in [cnt_masks(r)[rank - r - 1]]))
             for r in range(rank):
-                mm = E.matmul(T.pp[:, 0:1], T.ones[:], T.cnt[:, r:r + 1], False, r == rank - 1)
+                mm = E.matmul(pp, T.ones[:], T.cnt[:, r:r + 1], False, r == rank - 1)
         mm.then_inc(sem.e_p, 1)
 
+        A.wait_ge(sem.e_m, 3)
+        A.wait_ge(sem.gc2, 2)
+        A.activation(T.va[:], T.ia[:], IDENT, scale=ma).then_inc(sem.e_va, 1)
+        A.activation(T.vb[:], T.ib[:], IDENT, bias=mc, scale=mb).then_inc(sem.e_va, 1)
+
+        v(V.memset(T.ww[:, 0:TOK], 0.0))
+        V.wait_ge(sem.gc4, 1)
+        v(V.tensor_scalar(d1, dd, 1.0, None, ADD))
         V.wait_ge(sem.e_s, 1)
+        vw()
         v(V.tensor_tensor(at_, sc, d1, SUB))
-        shr, band, eq = AluOpType.arith_shift_right, AluOpType.bitwise_and, AluOpType.is_equal
-        v(V.tensor_scalar(krow, kk, 3, None, shr))
-        v(V.tensor_scalar(kg, kk, 7, None, band))
-        v(V.tensor_scalar(k16, kk, 15, None, band))
-        v(V.tensor_scalar(grp, kk, 4, None, shr))
         vw()
         v(V.tensor_tensor(ab, at_, kf, MUL))
-        v(V.tensor_copy(krowf, krow))
-        v(V.tensor_copy(kgf, kg))
-        v(V.tensor_scalar(ma, k16, 0.0, None, eq))
-        v(V.tensor_scalar(mb, k16, 1.0, None, eq))
-        v(V.tensor_scalar(m2, k16, 2.0, None, eq))
-        v(V.tensor_scalar(c2, grp, 2.0, 4.0, MUL, ADD))
         vw()
         v(V.tensor_tensor(av, ab, dd, ADD))
-        v(V.tensor_tensor(mc, m2, c2, MUL))
-        v(V.tensor_scalar(jc, kgf, 256.0, krowf, MUL, ADD))
-        V.wait_ge(sem.gc2, 2)
-        v(V.tensor_scalar(T.va[:], T.ia[:], ma, None, MUL))
-        vw()
-        v(V.tensor_scalar(T.vb[:], T.ib[:], mb, mc, MUL, ADD))
-        vw()
+        V.wait_ge(sem.e_va, 2)
         v(V.tensor_tensor(T.vv[:], T.va[:], T.vb[:], ADD))
+        V.memset(T.xg[:, 0:ZC], 0.0).then_inc(sem.e_z, 1)
         V.wait_ge(sem.e_p, 1)
-        v(V.tensor_scalar(T.off[:], av, T.pp[:, 0:1], None, ADD))
+        vw()
+        v(V.tensor_scalar(T.off[:], av, pp, None, ADD))
         vw()
         V.tensor_copy(T.ww[:, 0:WIN].indirect(T.off[:, 0:16]), T.vv[:]).then_inc(sem.e_w, 1)
 
+        halves = [order[0] // 2, 1 - order[0] // 2]
         E.wait_ge(sem.e_w, 1)
-        for a in range(16):
-            mm = E.matmul(T.hb0[:, 0:128], T.ee[:, 16 - a:144 - a], T.ww[:, a:TOK:16], a == 0, a == 15)
-        mm.then_inc(sem.e_l, 1)
-        V.wait_ge(sem.e_l, 1)
-        V.tensor_copy(T.lst[:], T.hb0[:, 0:128]).then_inc(sem.e_lst, 1)
+        for h, bank in zip(halves, (T.hb0, T.hb1)):
+            for a in range(16):
+                mm = E.matmul(bank[:, 0:64], T.ee[:, 16 - a:144 - a], T.ww[:, 1024 * h + a:1024 * h + 1024:16], a == 0, a == 15)
+            mm.then_inc(sem["e_l%d" % h], 1)
 
-        for q in (V, A):
-            q.wait_ge(sem.q_x, 16)
-            q.wait_ge(sem.e_z, 1)
-            q.wait_ge(sem.e_lst, 1)
         xw = T.xg[:, 0:XW]
+        seen = []
+        A.wait_ge(sem.q_x, 16)
+        A.wait_ge(sem.e_z, 1)
         for i, d in enumerate(order + [s]):
+            h = d // 2
+            if h not in seen:
+                seen.append(h)
+                V.wait_ge(sem["e_l%d" % h], 1)
+                V.tensor_copy(T.lst[:, 64 * h:64 * h + 64], (T.hb0 if h == halves[0] else T.hb1)[:, 0:64]).then_inc(sem["e_lst%d" % h], 1)
+                if len(seen) == 1:
+                    V.wait_ge(sem.q_x, 16)
+                    V.wait_ge(sem.e_z, 1)
+                for q in (V, A):
+                    q.wait_ge(sem["e_lst%d" % h], 1)
             c, l = CS * d, 32 * d
             V.tensor_copy(T.sb[:, c + 256:c + 512], xw.indirect(T.lst[:, l + 16:l + 32])).then_inc(sem["gv%d" % i], 1)
-            if d != s:
-                A.activation(T.sb[:, c:c + 256], xw.indirect(T.lst[:, l:l + 16]), COPY).then_inc(sem["ga%d" % i], 1)
-            else:
-                A.activation(T.sb[:, c + 128:c + 256], xw.indirect(T.lst[:, l + 8:l + 16]), COPY).then_inc(sem["ga%d" % i], 1)
-                A.activation(T.lnd[:, s * BL:s * BL + BL], xw.indirect(T.lst[:, l:l + 8]), COPY).then_inc(sem.e_own, 1)
+            A.activation(T.sb[:, c:c + 256], xw.indirect(T.lst[:, l:l + 16]), COPY).then_inc(sem["ga%d" % i], 1)
+
+        def share(buf, rsem, to):
+            send([tr(buf[:, CS * k:CS * k + CS], buf[:, 0:CS], [ws[k]], rsem, e) for k, e in to])
 
         g.wait_ge(sem.q_w1a, 16)
-        send([tr(T.w1s[:, CS * k:CS * k + CS], T.w1s[:, 0:CS], [ws[k]], sem.w1_in, full[4 * k - 4:4 * k]) for k in (1, 2, 3)])
+        send([tr(T.w1s[:, BL * t:BL * t + 768], T.w1s[:, 0:768], [ws[k]], sem.w1_in, e)
+              for k, t, e in ((1, 4, full[0:8]), (3, 10, full[8:16]))])
         for i, d in enumerate(order):
             c = CS * d
-            _, od = plan(T, topo, d)
+            _, _, od = plan(T, topo, d)
             g.wait_ge(sem["gv%d" % i], 1)
-            send([tr(T.sb[:, c + 256:c + 512], T.rl[:, 256 * i:256 * i + 256], [owners[2]], sem["rl_in%d" % i], up)])
+            send([tr(T.sb[:, c + 256 + BL * o:c + 256 + BL * o + BL], T.rl[:, BL * i:BL * i + BL], [ports[2 + o]],
+                     sem["rl_in%d" % i], up[4 * o:4 * o + 4]) for o in (0, 1)])
             g.wait_ge(sem["ga%d" % i], 1)
-            send([tr(T.sb[:, c + BL * o:c + BL * o + BL], T.lnd[:, s * BL:s * BL + BL], [od[o]], sem.fw, low[4 * o:4 * o + 4])
-                  for o in (0, 1)])
+            send([tr(T.sb[:, c + BL * o:c + BL * o + BL], T.lnd[:, s * BL:s * BL + BL], [od[o]], sem["fw%d" % i],
+                     low[4 * o:4 * o + 4]) for o in (0, 1)])
         g.wait_ge(sem.gv3, 1)
         g.wait_ge(sem.ga3, 1)
         c = CS * s
-        send([tr(T.sb[:, c + BL * o:c + BL * o + BL], T.lnd[:, s * BL:s * BL + BL], [owners[o]], sem.fw, full[4 * o:4 * o + 4])
-              for o in (1, 2, 3)])
+        send([tr(T.sb[:, c + BL * o:c + BL * o + BL], T.lnd[:, s * BL:s * BL + BL], [adders[o]], sem.fw3, full[4 * o:4 * o + 4])
+              for o in range(4)])
+        g.sem_inc(sem.go, 1)
         g.wait_ge(sem.q_w1b, 16)
-        send([tr(T.w1s[:, CS * k:CS * k + CS], T.w1s[:, 0:CS], [ws[k]], sem.w1_in, up[2 * k - 8:2 * k - 6]) for k in (4, 5, 6, 7)])
+        share(T.w1s, sem.w1_in, [(k, full[4 * k - 16:4 * k - 12]) for k in (4, 5, 6, 7)])
         g.wait_ge(sem.q_w2a, 16)
-        send([tr(T.w2s[:, CS * k:CS * k + CS], T.w2s[:, 0:CS], [ws[k]], sem.w2_in, up[2 * k:2 * k + 2]) for k in (1, 2, 3)])
+        share(T.w2s, sem.w2_in, [(1, full[0:8]), (2, full[8:12]), (3, full[12:16])])
         g.wait_ge(sem.q_w2b, 16)
-        send([tr(T.w2s[:, CS * k:CS * k + CS], T.w2s[:, 0:CS], [ws[k]], sem.w2_in, low[2 * k - 8:2 * k - 6]) for k in (4, 5, 6, 7)])
+        share(T.w2s, sem.w2_in, [(k, full[4 * k - 16:4 * k - 12]) for k in (4, 5, 6, 7)])
 
         V.wait_ge(sem.gc3, 3)
+        v(V.tensor_scalar(krow, kk, 3, None, shr))
+        v(V.tensor_scalar(kg, kk, 7, None, band))
+        v(V.tensor_scalar(f0, sc, pp, float(XW - 1), ADD, ADD))
+        vw()
+        v(V.tensor_copy(krowf, krow))
+        v(V.tensor_copy(kgf, kg))
+        vw()
+        v(V.tensor_scalar(jc, kgf, 256.0, krowf, MUL, ADD))
         v(V.tensor_scalar(T.r16[:], T.i16[:], krowf, None, eq))
         v(V.tensor_scalar(T.gm[:], T.i8[:], kgf, None, eq))
+        vw()
         v(V.tensor_scalar(j4, jj, jc, None, ADD))
-        v(V.tensor_scalar(f0, sc, T.pp[:, 0:1], float(XW - 1), ADD, ADD))
         vw()
         v(V.tensor_tensor(f1, f0, j4, SUB))
         vw()
@@ -274,139 +296,170 @@ def rank_program(g, core, T, topo):
         vw()
         for i in range(8):
             V.tensor_scalar(T.fr[:, 16 * i:16 * i + 16], f3, T.gm[:, i:i + 1], None, MUL).then_inc(sem.e_fr, 1)
+        for h in (0, 1):
+            E.wait_ge(sem["e_lst%d" % h], 1)
         E.wait_ge(sem.e_fr, 8)
-        E.matmul(T.hb1[:, 0:128], T.r16[:], T.fr[:], True, True).then_inc(sem.e_fp, 1)
+        E.matmul(T.yb2[:, 0:128], T.r16[:], T.fr[:], True, True).then_inc(sem.e_fp, 1)
         V.wait_ge(sem.e_fp, 1)
-        V.tensor_copy(T.fo[:], T.hb1[:, 0:128]).then_inc(sem.e_fo, 1)
-        E.wait_ge(sem.e_lst, 1)
-        E.wait_ge(sem.e_fo, 1)
+        V.tensor_copy(T.fo[:], T.yb2[:, 0:128]).then_inc(sem.e_fo, 1)
 
-    if own == 2:
+    if core in ports[2:]:
+        o = ports.index(core)
         for i, d in enumerate(order):
-            _, od = plan(T, topo, d)
-            g.wait_ge(sem["rl_in%d" % i], 8)
-            send([tr(T.rl[:, 256 * i + BL * o:256 * i + BL * o + BL], T.lnd[:, s * BL:s * BL + BL], [od[2 + o]], sem.fw,
-                     low[4 * o:4 * o + 4]) for o in (0, 1)])
+            _, _, od = plan(T, topo, d)
+            g.wait_ge(sem["rl_in%d" % i], 4)
+            send([tr(T.rl[:, BL * i:BL * i + BL], T.lnd[:, s * BL:s * BL + BL], [od[o]], sem["fw%d" % i], low)])
 
-    if own is not None:
-        p = POS[own]
-        V.wait_ge(sem.fw, 12 if is_r else 16)
-        if is_r:
-            V.wait_ge(sem.e_own, 1)
-        v(V.tensor_tensor(T.ta[:], T.lnd[:, 0:BL], T.lnd[:, BL:2 * BL], ADD))
-        v(V.tensor_tensor(T.tb[:], T.lnd[:, 2 * BL:3 * BL], T.lnd[:, 3 * BL:4 * BL], ADD))
-        vw()
+    if core in adders:
+        p = adders.index(core)
+        n = 4 if p < 2 else 8
+        if p < 2:
+            g.wait_ge(sem.w1_in, 8)
+            c, to = (0, 256) if p else (512, 0)
+            send([tr(T.w1s[:, c:c + 256], T.w1s[:, to:to + 256], [ws[2]], sem.w1_in, full)])
+
+        def blk_of(i):
+            r = (s - 1 - i) % N
+            return T.lnd[:, r * BL:r * BL + BL]
         blk = T.xc[:, p * BL:p * BL + BL]
-        V.tensor_tensor(blk, T.ta[:], T.tb[:], ADD).then_inc(sem.e_x, 1)
+        V.wait_ge(sem.fw0, n)
+        V.wait_ge(sem.fw1, n)
+        v(V.tensor_tensor(T.ta[:], blk_of(0), blk_of(1), ADD))
+        V.wait_ge(sem.fw3, 4)
+        vw()
+        v(V.tensor_tensor(T.tb[:], T.ta[:], blk_of(3), ADD))
+        V.wait_ge(sem.fw2, n)
+        vw()
+        V.tensor_tensor(blk, T.tb[:], blk_of(2), ADD).then_inc(sem.e_x, 1)
         g.wait_ge(sem.e_x, 1)
-        send([tr(blk, blk, [c for c in ws if c != core], sem["xc%d" % (p // 2)], full)])
+        send([tr(blk, blk, [c for c in ws if c != core], sem["xc%d" % p], full)])
 
     hb = [T.hb0, T.hb1, T.hb2, T.hb3]
-    yb = [T.yb0, T.yb1]
+    yb = [T.yb0, T.yb1, T.yb2, T.yb3]
+    w1at = 256 if core == adders[1] else 0
 
-    def layer1(n):
-        h, i = n // 4, n % 4
-        if i == 0:
-            others = [c for c in owner_at[2 * h:2 * h + 2] if c != core]
-            E.wait_ge(sem["xc%d" % h], 16 * len(others))
-            if len(others) == 1:
-                E.wait_ge(sem.e_x, 1)
-        E.matmul(hb[n % 4][:, 0:256], T.w1s[:, 128 * i:128 * i + 128], T.xc[:, 256 * h:256 * h + 256], True, True).then_inc(sem["ha%d" % n], 1)
-        hs = T.hh[:, 256 * n:256 * n + 256]
-        if n % 2 == 0:
-            A.wait_ge(sem["ha%d" % n], 1)
-            A.activation(hs, hb[n % 4][:, 0:256], RELU).then_inc(sem["hr%d" % n], 1)
+    def layer1(q):
+        if core == adders[q]:
+            E.wait_ge(sem.e_x, 1)
         else:
-            V.wait_ge(sem["ha%d" % n], 1)
-            V.tensor_scalar(hs, hb[n % 4][:, 0:256], 0.0, None, MAX).then_inc(sem["hr%d" % n], 1)
+            E.wait_ge(sem["xc%d" % q], 16)
+        for b in (0, 1):
+            bank = hb[2 * (q % 2) + b]
+            k = 2 * q + b
+            if q >= 2:
+                E.wait_ge(sem["hr%d" % (k - 4)], 1)
+            for i in (0, 1):
+                w = w1at + BL * (2 * b + i)
+                E.matmul(bank[:, BL * i:BL * i + BL], T.w1s[:, w:w + BL], T.xc[:, BL * q:BL * q + BL],
+                         True, True).then_inc(sem["ha%d" % k], 1)
+            hs = T.hh[:, CS * q + 256 * b:CS * q + 256 * b + 256]
+            if b == 0:
+                A.wait_ge(sem["ha%d" % k], 2)
+                A.activation(hs, bank[:, 0:256], RELU).then_inc(sem["hr%d" % k], 1)
+            else:
+                V.wait_ge(sem["ha%d" % k], 2)
+                V.tensor_scalar(hs, bank[:, 0:256], 0.0, None, MAX).then_inc(sem["hr%d" % k], 1)
 
-    def layer2(n):
-        h, i = n // 4, n % 4
-        E.wait_ge(sem["hr%d" % n], 1)
-        m = E.matmul(yb[h][:, 0:256], T.w2s[:, 128 * i:128 * i + 128], T.hh[:, 256 * n:256 * n + 256], i == 0, i == 3)
-        if i == 3:
-            m.then_inc(sem["e_y%d" % h], 1)
+    def layer2(q):
+        for t in range(4):
+            if t % 2 == 0:
+                E.wait_ge(sem["hr%d" % (2 * q + t // 2)], 1)
+            m = E.matmul(yb[q][:, 0:BL], T.w2s[:, BL * t:BL * t + BL], T.hh[:, CS * q + BL * t:CS * q + BL * t + BL], t == 0, t == 3)
+        m.then_inc(sem["e_y%d" % q], 1)
 
-    def home(h):
-        q = A if h else V
-        q.wait_ge(sem["e_y%d" % h], 1)
-
-        def copy(out, in_):
-            return A.activation(out, in_, COPY) if h else V.tensor_copy(out, in_)
-        pair = owner_at[2 * h:2 * h + 2]
-        c = 256 * h
+    def home(q):
+        A.wait_ge(sem["e_y%d" % q], 1)
+        pair = [ports[q % 2], ports[2 + q % 2]]
+        c, base = BL * q, 8 * HB * (q // 2)
+        land = T.red[:, base + me * HB:base + me * HB + HB]
         if core in pair:
             b = pair.index(core)
             o = 1 - b
-            copy(T.yp[:, c + BL * o:c + BL * o + BL], yb[h][:, BL * o:BL * o + BL]).then_inc(sem["e_ev%d" % h], 1)
-            copy(T.red[:, me * BL:me * BL + BL], yb[h][:, BL * b:BL * b + BL]).then_inc(sem.e_so, 1)
+            A.activation(T.yp[:, c + HB * o:c + HB * o + HB], yb[q][:, HB * o:HB * o + HB], COPY).then_inc(sem["e_ev%d" % q], 1)
+            A.activation(land, yb[q][:, HB * b:HB * b + HB], COPY).then_inc(sem["e_so%d" % (q // 2)], 1)
             todo = [(o, full)]
         else:
-            copy(T.yp[:, c:c + 256], yb[h][:, 0:256]).then_inc(sem["e_ev%d" % h], 1)
+            A.activation(T.yp[:, c:c + BL], yb[q][:, 0:BL], COPY).then_inc(sem["e_ev%d" % q], 1)
             todo = [(0, full[0:8]), (1, full[8:16])]
-        g.wait_ge(sem["e_ev%d" % h], 1)
-        send([tr(T.yp[:, c + BL * o:c + BL * o + BL], T.red[:, me * BL:me * BL + BL], [pair[o]], sem.rd, e) for o, e in todo])
+        g.wait_ge(sem["e_ev%d" % q], 1)
+        send([tr(T.yp[:, c + HB * o:c + HB * o + HB], land, [pair[o]], sem["rd%d" % (q // 2)], e) for o, e in todo])
 
-    def collect():
-        V.wait_ge(sem.rd, 6 * 8 + 16)
-        V.wait_ge(sem.e_so, 1)
-        v(V.tensor_tensor(T.t4[:], T.red[:, 0:512], T.red[:, 512:1024], ADD))
-        vw()
-        v(V.tensor_tensor(T.t2[:], T.t4[:, 0:256], T.t4[:, 256:512], ADD))
-        vw()
-        at = XW + CS * s + BL * own
-        out = T.xg[:, at:at + BL] if is_r else T.sm[:]
-        V.tensor_tensor(out, T.t2[:, 0:128], T.t2[:, 128:256], ADD).then_inc(sem.e_red, 1)
+    own = ports.index(core) if core in ports else None
 
-    def deliver():
-        at = XW + CS * s + BL * own
-        slot = T.xg[:, at:at + BL]
-        out = slot if is_r else T.sm[:]
-        g.wait_ge(sem.e_red, 1)
+    def result(k):
+        q, h = 2 * k + own % 2, own // 2
+        at = XW + CS * s + BL * q + HB * h
+        slot = T.xg[:, at:at + HB]
+        return slot, (slot if is_r else T.sm[:, HB * k:HB * k + HB])
+
+    def collect(k):
+        if own is None:
+            return
+        V.wait_ge(sem["rd%d" % k], 6 * 8 + 16)
+        V.wait_ge(sem["e_so%d" % k], 1)
+        r, f, w = 8 * HB * k, 4 * HB * k, 2 * HB * k
+        v(V.tensor_tensor(T.t4[:, f:f + 4 * HB], T.red[:, r:r + 4 * HB], T.red[:, r + 4 * HB:r + 8 * HB], ADD))
+        vw()
+        v(V.tensor_tensor(T.t2[:, w:w + 2 * HB], T.t4[:, f:f + 2 * HB], T.t4[:, f + 2 * HB:f + 4 * HB], ADD))
+        vw()
+        V.tensor_tensor(result(k)[1], T.t2[:, w:w + HB], T.t2[:, w + HB:w + 2 * HB], ADD).then_inc(sem["e_red%d" % k], 1)
+
+    def deliver(k):
+        if own is None:
+            return
+        slot, out = result(k)
+        g.wait_ge(sem["e_red%d" % k], 1)
         trs = [tr(out, slot, [T.cores[d] for d in order], sem.gg, low)]
         if not is_r:
             trs.append(tr(out, slot, [R], sem.gg, up))
         send(trs)
 
-    if not is_r:
-        E.wait_ge(sem.w1_in, 4 if me < 4 else 2)
-    else:
+    if is_r:
         E.wait_ge(sem.q_w1a, 16)
+    else:
+        E.wait_ge(sem.w1_in, 4 if me > 3 else 32 if me == 2 else 8)
     layer1(0)
     layer1(1)
-    if not is_r:
-        E.wait_ge(sem.w2_in, 2)
-    else:
+    if is_r:
         E.wait_ge(sem.q_w2a, 16)
-    for n in range(8):
-        layer2(n)
-        if n + 2 < 8:
-            layer1(n + 2)
-        if n == 3:
-            home(0)
-    early = own is not None and POS[own] < 2
-    if early:
-        collect()
+        E.wait_ge(sem.e_fo, 1)
+    else:
+        E.wait_ge(sem.w2_in, 8 if me == 1 else 4)
+    layer2(0)
+    home(0)
+    layer1(2)
+    layer2(1)
     home(1)
-    if own is not None:
-        if not early:
-            collect()
-        deliver()
+    layer1(3)
+    collect(0)
+    layer2(2)
+    if own is not None and own % 2 == 0:
+        deliver(0)
+        home(2)
+    else:
+        home(2)
+        deliver(0)
+    layer2(3)
+    home(3)
+    collect(1)
+    deliver(1)
 
     if is_r:
         for q in (V, A):
-            q.wait_ge(sem.gg, 15 * 8)
-            q.wait_ge(sem.e_red, 1)
+            q.wait_ge(sem.gg, 2 * 15 * 8)
+            q.wait_ge(sem.e_red0, 1)
+            q.wait_ge(sem.e_red1, 1)
             q.wait_ge(sem.e_fo, 1)
-        for c in (0, 2, 1, 3):
-            src = T.xg[:].indirect(T.fo[:, 32 * c:32 * c + 32])
-            out = T.yo[:, CS * c:CS * c + CS]
-            ins = V.tensor_copy(out, src) if c < 2 else A.activation(out, src, COPY)
-            ins.then_inc(sem["fin%d" % c], 1)
-        for c in (0, 2, 1, 3):
-            Y.wait_ge(sem["fin%d" % c], 1)
-            Y.dma_start(T.y[:, CS * c:CS * c + CS], T.yo[:, CS * c:CS * c + CS]).then_inc(sem.q_y, 16)
-        Y.wait_ge(sem.q_y, 64)
+        pieces = [(0, 512, V), (1024, 512, A), (512, 256, V), (1536, 256, A), (768, 256, V), (1792, 256, A)]
+        for i, (c, n, q) in enumerate(pieces):
+            src = T.xg[:].indirect(T.fo[:, c // 16:(c + n) // 16])
+            out = T.yo[:, c:c + n]
+            ins = V.tensor_copy(out, src) if q is V else A.activation(out, src, COPY)
+            ins.then_inc(sem["fin%d" % i], 1)
+        for i, (c, n, q) in enumerate(pieces):
+            Y.wait_ge(sem["fin%d" % i], 1)
+            Y.dma_start(T.y[:, c:c + n], T.yo[:, c:c + n]).then_inc(sem.q_y, 16)
+        Y.wait_ge(sem.q_y, 16 * len(pieces))
 
     vw()
     if nls[0]:

from concourse.bass import DstId, RemoteDMATransfer
from concourse.mybir import AluOpType, ActivationFunctionType

N = 4
CORES_SIM = 112
TOK = 2048
CS = 512
BL = 128
HB = 64
ZC = 4
XW = ZC + TOK
WIN = 3 * TOK

SCRATCH = {
    "k2": ("sbuf", [128, 16], "int32"),
    "s16": ("sbuf", [128, 256], "float32"),
    "off": ("sbuf", [128, 16], "uint16"),
    "cnt": ("sbuf", [128, 4], "float32"),
    "ki": ("sbuf", [128, 8], "int32"),
    "kc": ("sbuf", [128, 16], "float32"),
    "tri": ("sbuf", [128, 128], "float32"),
    "ones": ("sbuf", [128, 128], "float32"),
    "ee": ("sbuf", [128, 144], "bfloat16"),
    "ia": ("sbuf", [128, 256], "float32"),
    "ib": ("sbuf", [128, 256], "float32"),
    "va": ("sbuf", [128, 256], "float32"),
    "vb": ("sbuf", [128, 256], "float32"),
    "vv": ("sbuf", [128, 256], "bfloat16"),
    "ww": ("sbuf", [128, WIN], "bfloat16"),
    "lst": ("sbuf", [128, 128], "uint16"),
    "i16": ("sbuf", [128, 128], "float32"),
    "r16": ("sbuf", [128, 128], "float32"),
    "i8": ("sbuf", [128, 8], "float32"),
    "gm": ("sbuf", [128, 8], "float32"),
    "fr": ("sbuf", [128, 128], "float32"),
    "fo": ("sbuf", [128, 128], "uint16"),
    "xg": ("sbuf", [128, XW + TOK], "float32"),
    "sb": ("sbuf", [128, TOK], "float32"),
    "rl": ("sbuf", [128, 3 * BL], "float32"),
    "lnd": ("sbuf", [128, N * BL], "float32"),
    "ta": ("sbuf", [128, BL], "float32"),
    "tb": ("sbuf", [128, BL], "float32"),
    "xc": ("sbuf", [128, CS], "float32"),
    "w1s": ("sbuf", [128, 4096], "float32"),
    "w2s": ("sbuf", [128, 4096], "float32"),
    "hh": ("sbuf", [128, 2048], "float32"),
    "yp": ("sbuf", [128, CS], "float32"),
    "red": ("sbuf", [128, 2 * 8 * HB], "float32"),
    "t4": ("sbuf", [128, 2 * 4 * HB], "float32"),
    "t2": ("sbuf", [128, 2 * 2 * HB], "float32"),
    "sm": ("sbuf", [128, 2 * HB], "float32"),
    "yo": ("sbuf", [128, TOK], "float32"),
    "hb0": ("psum", [128, 512], "float32"),
    "hb1": ("psum", [128, 512], "float32"),
    "hb2": ("psum", [128, 512], "float32"),
    "hb3": ("psum", [128, 512], "float32"),
    "yb0": ("psum", [128, 512], "float32"),
    "yb1": ("psum", [128, 512], "float32"),
    "yb2": ("psum", [128, 512], "float32"),
    "yb3": ("psum", [128, 512], "float32"),
}
SEMAPHORES = (["q_keep", "q_x", "q_w1a", "q_w1b", "q_w2a", "q_w2b", "q_y", "go",
               "gc1", "gc2", "gc3", "gc4", "e_k", "e_o", "e_m", "e_va", "vs", "e_z", "e_s", "e_p", "e_w", "e_fr", "e_fp", "e_fo",
               "e_x", "cnt_in", "w1_in", "w2_in", "gg", "ls", "lc"]
              + ["%s%d" % (n, i) for n in ("gv", "ga", "fw", "rl_in", "xc", "e_y", "e_ev", "e_so") for i in range(4)]
              + ["%s%d" % (n, i) for n in ("e_l", "e_lst", "rd", "e_red") for i in range(2)]
              + ["%s%d" % (n, i) for n in ("ha", "hr") for i in range(8)] + ["fin%d" % i for i in range(6)])

ADD, SUB, MUL, MAX = AluOpType.add, AluOpType.subtract, AluOpType.mult, AluOpType.max
COPY, RELU, IDENT = ActivationFunctionType.Copy, ActivationFunctionType.Relu, ActivationFunctionType.Identity


def bits(m):
    return [1 << i for i in range(16) if m >> i & 1]


def plan(T, topo, s):
    R = T.cores[s]
    cs = [c for c in range(CORES_SIM) if topo.chip(c) == topo.chip(R)]
    ports = [c for c in cs if all(topo.may_write(c, d) for d in T.cores if d != c)]
    near = [c for c in ports if topo.die(c) == topo.die(R) and c != R]
    far = [c for c in ports if topo.die(c) != topo.die(R)]
    rest = [c for c in cs if c not in ports]
    adders = [c for c in rest if topo.die(c) == topo.die(R)] + [c for c in rest if topo.die(c) != topo.die(R)]
    ws = [R, adders[0], near[0], adders[1], adders[2], far[0], adders[3], far[1]]
    return ws, [R, near[0], far[0], far[1]], adders


def rank_program(g, core, T, topo):
    chip_of = [s for s in range(N) if topo.chip(T.cores[s]) == topo.chip(core)]
    if not chip_of:
        return
    s = chip_of[0]
    ws, ports, adders = plan(T, topo, s)
    R = ws[0]
    me = ws.index(core)
    is_r = core == R
    order = [(s + i) % N for i in range(1, N)]
    V, A, E, Y, sem = g.vector, g.scalar, g.tensor, g.sync, T.sem
    full = bits(topo.mask(core, ws[1] if is_r else R))
    low = bits(topo.mask(core, T.cores[order[0]]))
    up = [b for b in full if b not in low]
    nls = [0]
    nvs = [0]

    def dst(c):
        rid, pid, _ = topo.addr(c)
        return DstId(rid=rid, pnc=pid)

    def tr(src, out, to, rsem, eng):
        nls[0] += len(eng)
        return RemoteDMATransfer(dst_ids=[dst(c) for c in to], dma_engine_mask=sum(eng), remote_sem=rsem,
                                 srcs=[src], dsts=[out for _ in to], alu_op=0)

    def send(trs):
        g.remote_dma_fused(trs, local_sem=sem.ls)

    def v(ins):
        ins.then_inc(sem.vs, 1)
        nvs[0] += 1

    def vw():
        if nvs[0]:
            V.wait_ge(sem.vs, nvs[0])

    def cnt_masks(r):
        n = N - 1 - r
        return {1: [(0, 8)], 2: [(0, 4), (4, 8)], 3: [(0, 2), (2, 4), (4, 8)]}.get(n, [])

    if is_r:
        rank = s
        kk, krow, kg, k16, grp = [T.ki[:, i:i + 1] for i in range(5)]
        krowf, kgf, ma, mb, m2, c2, mc, jc = [T.kc[:, i:i + 1] for i in range(8)]
        kf, sc, dd, d1, at_, ab, av, z16, jj, j4, f0, f1, f2, f3 = [T.s16[:, 16 * i:16 * i + 16] for i in range(14)]
        last = T.s16[:, 31:32]
        pp = T.yb3[:, 0:1]
        shr, band, eq = AluOpType.arith_shift_right, AluOpType.bitwise_and, AluOpType.is_equal
        later = list(range(rank + 1, N))
        Y.dma_start(T.k2[:], T.keep[:]).then_inc(sem.q_keep, 16)
        Y.dma_start(T.xg[:, ZC:XW], T.x[:]).then_inc(sem.q_x, 16)
        Y.dma_start(T.w1s[:, 0:2048], T.w1[:, 0:2048]).then_inc(sem.q_w1a, 16)
        if later:
            Y.wait_ge(sem.lc, sum(b - a for a, b in cnt_masks(rank)))
        else:
            Y.wait_ge(sem.q_w1a, 16)
        Y.dma_start(T.w1s[:, 2048:4096], T.w1[:, 2048:4096]).then_inc(sem.q_w1b, 16)
        Y.wait_ge(sem.q_w1b, 16)
        Y.dma_start(T.w2s[:, 0:2048], T.w2[:, 0:2048]).then_inc(sem.q_w2a, 16)
        Y.wait_ge(sem.go, 1)
        Y.dma_start(T.w2s[:, 2048:4096], T.w2[:, 2048:4096]).then_inc(sem.q_w2b, 16)

        ok = {"allow_small_or_imprecise_dtypes": True}
        g.iota(kk, [[0, 1]], 0, 1).then_inc(sem.gc1, 1)
        g.iota(T.ia[:], [[0, 16], [0, 2], [256, 8]], 0, 0, **ok).then_inc(sem.gc2, 1)
        g.iota(T.ib[:], [[16, 16], [1, 2], [0, 8]], 0, 0, **ok).then_inc(sem.gc2, 1)
        g.wait_ge(sem.e_o, 1)
        g.affine_select(T.tri[:], T.ones[:], [[1, 128]], AluOpType.is_gt, 0.0, 0, -1).then_inc(sem.e_k, 1)

        V.memset(T.ones[:], 1.0).then_inc(sem.e_o, 1)
        v(V.memset(z16, 0.0))
        v(V.memset(T.ee[:], 0.0))
        V.wait_ge(sem.gc1, 1)
        v(V.tensor_scalar(k16, kk, 15, None, band))
        v(V.tensor_scalar(grp, kk, 4, None, shr))
        vw()
        V.memset(T.ee[:, 0:144:16], 1.0).then_inc(sem.e_k, 1)
        v(V.tensor_scalar(m2, k16, 2.0, None, eq))
        v(V.tensor_scalar(c2, grp, 2.0, 4.0, MUL, ADD))
        V.tensor_scalar(ma, k16, 0.0, None, eq).then_inc(sem.e_m, 1)
        V.tensor_scalar(mb, k16, 1.0, None, eq).then_inc(sem.e_m, 1)
        vw()
        V.tensor_tensor(mc, m2, c2, MUL).then_inc(sem.e_m, 1)

        V.wait_ge(sem.q_keep, 16)
        v(V.tensor_copy(kf, T.k2[:]))
        vw()
        V.tensor_tensor_scan(sc, kf, z16, 0.0, ADD, ADD).then_inc(sem.e_s, 1)

        if later:
            g.wait_ge(sem.e_s, 1)
            g.remote_dma_fused([tr(last, T.cnt[:, rank:rank + 1], [T.cores[d]], sem.cnt_in, low[a:b])
                                for d, (a, b) in zip(later, cnt_masks(rank))], local_sem=sem.lc)
            nls[0] = 0
        g.iota(dd, [[1, 16]], TOK, 16, **ok).then_inc(sem.gc4, 1)
        g.iota(T.i16[:], [[0, 8], [1, 16]], 0, 0, **ok).then_inc(sem.gc3, 1)
        g.iota(T.i8[:], [[1, 8]], 0, 0, **ok).then_inc(sem.gc3, 1)
        g.iota(jj, [[16, 16]], ZC, 0, **ok).then_inc(sem.gc3, 1)

        E.wait_ge(sem.e_k, 2)
        E.wait_ge(sem.e_o, 1)
        E.wait_ge(sem.e_s, 1)
        mm = E.matmul(pp, T.tri[:], last, True, rank == 0)
        if rank:
            E.wait_ge(sem.cnt_in, sum(b - a for r in range(rank) for a, b in [cnt_masks(r)[rank - r - 1]]))
            for r in range(rank):
                mm = E.matmul(pp, T.ones[:], T.cnt[:, r:r + 1], False, r == rank - 1)
        mm.then_inc(sem.e_p, 1)

        A.wait_ge(sem.e_m, 3)
        A.wait_ge(sem.gc2, 2)
        A.activation(T.va[:], T.ia[:], IDENT, scale=ma).then_inc(sem.e_va, 1)
        A.activation(T.vb[:], T.ib[:], IDENT, bias=mc, scale=mb).then_inc(sem.e_va, 1)

        v(V.memset(T.ww[:, 0:TOK], 0.0))
        V.wait_ge(sem.gc4, 1)
        v(V.tensor_scalar(d1, dd, 1.0, None, ADD))
        V.wait_ge(sem.e_s, 1)
        vw()
        v(V.tensor_tensor(at_, sc, d1, SUB))
        vw()
        v(V.tensor_tensor(ab, at_, kf, MUL))
        vw()
        v(V.tensor_tensor(av, ab, dd, ADD))
        V.wait_ge(sem.e_va, 2)
        v(V.tensor_tensor(T.vv[:], T.va[:], T.vb[:], ADD))
        V.memset(T.xg[:, 0:ZC], 0.0).then_inc(sem.e_z, 1)
        V.wait_ge(sem.e_p, 1)
        vw()
        v(V.tensor_scalar(T.off[:], av, pp, None, ADD))
        vw()
        V.tensor_copy(T.ww[:, 0:WIN].indirect(T.off[:, 0:16]), T.vv[:]).then_inc(sem.e_w, 1)

        halves = [order[0] // 2, 1 - order[0] // 2]
        E.wait_ge(sem.e_w, 1)
        for h, bank in zip(halves, (T.hb0, T.hb1)):
            for a in range(16):
                mm = E.matmul(bank[:, 0:64], T.ee[:, 16 - a:144 - a], T.ww[:, 1024 * h + a:1024 * h + 1024:16], a == 0, a == 15)
            mm.then_inc(sem["e_l%d" % h], 1)

        xw = T.xg[:, 0:XW]
        seen = []
        A.wait_ge(sem.q_x, 16)
        A.wait_ge(sem.e_z, 1)
        for i, d in enumerate(order + [s]):
            h = d // 2
            if h not in seen:
                seen.append(h)
                V.wait_ge(sem["e_l%d" % h], 1)
                V.tensor_copy(T.lst[:, 64 * h:64 * h + 64], (T.hb0 if h == halves[0] else T.hb1)[:, 0:64]).then_inc(sem["e_lst%d" % h], 1)
                if len(seen) == 1:
                    V.wait_ge(sem.q_x, 16)
                    V.wait_ge(sem.e_z, 1)
                for q in (V, A):
                    q.wait_ge(sem["e_lst%d" % h], 1)
            c, l = CS * d, 32 * d
            V.tensor_copy(T.sb[:, c + 256:c + 512], xw.indirect(T.lst[:, l + 16:l + 32])).then_inc(sem["gv%d" % i], 1)
            A.activation(T.sb[:, c:c + 256], xw.indirect(T.lst[:, l:l + 16]), COPY).then_inc(sem["ga%d" % i], 1)

        def share(buf, rsem, to):
            send([tr(buf[:, CS * k:CS * k + CS], buf[:, 0:CS], [ws[k]], rsem, e) for k, e in to])

        g.wait_ge(sem.q_w1a, 16)
        send([tr(T.w1s[:, BL * t:BL * t + 768], T.w1s[:, 0:768], [ws[k]], sem.w1_in, e)
              for k, t, e in ((1, 4, full[0:8]), (3, 10, full[8:16]))])
        for i, d in enumerate(order):
            c = CS * d
            _, _, od = plan(T, topo, d)
            g.wait_ge(sem["gv%d" % i], 1)
            send([tr(T.sb[:, c + 256 + BL * o:c + 256 + BL * o + BL], T.rl[:, BL * i:BL * i + BL], [ports[2 + o]],
                     sem["rl_in%d" % i], up[4 * o:4 * o + 4]) for o in (0, 1)])
            g.wait_ge(sem["ga%d" % i], 1)
            send([tr(T.sb[:, c + BL * o:c + BL * o + BL], T.lnd[:, s * BL:s * BL + BL], [od[o]], sem["fw%d" % i],
                     low[4 * o:4 * o + 4]) for o in (0, 1)])
        g.wait_ge(sem.gv3, 1)
        g.wait_ge(sem.ga3, 1)
        c = CS * s
        send([tr(T.sb[:, c + BL * o:c + BL * o + BL], T.lnd[:, s * BL:s * BL + BL], [adders[o]], sem.fw3, full[4 * o:4 * o + 4])
              for o in range(4)])
        g.sem_inc(sem.go, 1)
        g.wait_ge(sem.q_w1b, 16)
        share(T.w1s, sem.w1_in, [(k, full[4 * k - 16:4 * k - 12]) for k in (4, 5, 6, 7)])
        g.wait_ge(sem.q_w2a, 16)
        share(T.w2s, sem.w2_in, [(1, full[0:8]), (2, full[8:12]), (3, full[12:16])])
        g.wait_ge(sem.q_w2b, 16)
        share(T.w2s, sem.w2_in, [(k, full[4 * k - 16:4 * k - 12]) for k in (4, 5, 6, 7)])

        V.wait_ge(sem.gc3, 3)
        v(V.tensor_scalar(krow, kk, 3, None, shr))
        v(V.tensor_scalar(kg, kk, 7, None, band))
        v(V.tensor_scalar(f0, sc, pp, float(XW - 1), ADD, ADD))
        vw()
        v(V.tensor_copy(krowf, krow))
        v(V.tensor_copy(kgf, kg))
        vw()
        v(V.tensor_scalar(jc, kgf, 256.0, krowf, MUL, ADD))
        v(V.tensor_scalar(T.r16[:], T.i16[:], krowf, None, eq))
        v(V.tensor_scalar(T.gm[:], T.i8[:], kgf, None, eq))
        vw()
        v(V.tensor_scalar(j4, jj, jc, None, ADD))
        vw()
        v(V.tensor_tensor(f1, f0, j4, SUB))
        vw()
        v(V.tensor_tensor(f2, f1, kf, MUL))
        vw()
        v(V.tensor_tensor(f3, f2, j4, ADD))
        vw()
        for i in range(8):
            V.tensor_scalar(T.fr[:, 16 * i:16 * i + 16], f3, T.gm[:, i:i + 1], None, MUL).then_inc(sem.e_fr, 1)
        for h in (0, 1):
            E.wait_ge(sem["e_lst%d" % h], 1)
        E.wait_ge(sem.e_fr, 8)
        E.matmul(T.yb2[:, 0:128], T.r16[:], T.fr[:], True, True).then_inc(sem.e_fp, 1)
        V.wait_ge(sem.e_fp, 1)
        V.tensor_copy(T.fo[:], T.yb2[:, 0:128]).then_inc(sem.e_fo, 1)

    if core in ports[2:]:
        o = ports.index(core)
        for i, d in enumerate(order):
            _, _, od = plan(T, topo, d)
            g.wait_ge(sem["rl_in%d" % i], 4)
            send([tr(T.rl[:, BL * i:BL * i + BL], T.lnd[:, s * BL:s * BL + BL], [od[o]], sem["fw%d" % i], low)])

    if core in adders:
        p = adders.index(core)
        n = 4 if p < 2 else 8
        if p < 2:
            g.wait_ge(sem.w1_in, 8)
            c, to = (0, 256) if p else (512, 0)
            send([tr(T.w1s[:, c:c + 256], T.w1s[:, to:to + 256], [ws[2]], sem.w1_in, full)])

        def blk_of(i):
            r = (s - 1 - i) % N
            return T.lnd[:, r * BL:r * BL + BL]
        blk = T.xc[:, p * BL:p * BL + BL]
        V.wait_ge(sem.fw0, n)
        V.wait_ge(sem.fw1, n)
        v(V.tensor_tensor(T.ta[:], blk_of(0), blk_of(1), ADD))
        V.wait_ge(sem.fw3, 4)
        vw()
        v(V.tensor_tensor(T.tb[:], T.ta[:], blk_of(3), ADD))
        V.wait_ge(sem.fw2, n)
        vw()
        V.tensor_tensor(blk, T.tb[:], blk_of(2), ADD).then_inc(sem.e_x, 1)
        g.wait_ge(sem.e_x, 1)
        send([tr(blk, blk, [c for c in ws if c != core], sem["xc%d" % p], full)])

    hb = [T.hb0, T.hb1, T.hb2, T.hb3]
    yb = [T.yb0, T.yb1, T.yb2, T.yb3]
    w1at = 256 if core == adders[1] else 0

    def layer1(q):
        if core == adders[q]:
            E.wait_ge(sem.e_x, 1)
        else:
            E.wait_ge(sem["xc%d" % q], 16)
        for b in (0, 1):
            bank = hb[2 * (q % 2) + b]
            k = 2 * q + b
            if q >= 2:
                E.wait_ge(sem["hr%d" % (k - 4)], 1)
            for i in (0, 1):
                w = w1at + BL * (2 * b + i)
                E.matmul(bank[:, BL * i:BL * i + BL], T.w1s[:, w:w + BL], T.xc[:, BL * q:BL * q + BL],
                         True, True).then_inc(sem["ha%d" % k], 1)
            hs = T.hh[:, CS * q + 256 * b:CS * q + 256 * b + 256]
            if b == 0:
                A.wait_ge(sem["ha%d" % k], 2)
                A.activation(hs, bank[:, 0:256], RELU).then_inc(sem["hr%d" % k], 1)
            else:
                V.wait_ge(sem["ha%d" % k], 2)
                V.tensor_scalar(hs, bank[:, 0:256], 0.0, None, MAX).then_inc(sem["hr%d" % k], 1)

    def layer2(q):
        for t in range(4):
            if t % 2 == 0:
                E.wait_ge(sem["hr%d" % (2 * q + t // 2)], 1)
            m = E.matmul(yb[q][:, 0:BL], T.w2s[:, BL * t:BL * t + BL], T.hh[:, CS * q + BL * t:CS * q + BL * t + BL], t == 0, t == 3)
        m.then_inc(sem["e_y%d" % q], 1)

    def home(q):
        A.wait_ge(sem["e_y%d" % q], 1)
        pair = [ports[q % 2], ports[2 + q % 2]]
        c, base = BL * q, 8 * HB * (q // 2)
        land = T.red[:, base + me * HB:base + me * HB + HB]
        if core in pair:
            b = pair.index(core)
            o = 1 - b
            A.activation(T.yp[:, c + HB * o:c + HB * o + HB], yb[q][:, HB * o:HB * o + HB], COPY).then_inc(sem["e_ev%d" % q], 1)
            A.activation(land, yb[q][:, HB * b:HB * b + HB], COPY).then_inc(sem["e_so%d" % (q // 2)], 1)
            todo = [(o, full)]
        else:
            A.activation(T.yp[:, c:c + BL], yb[q][:, 0:BL], COPY).then_inc(sem["e_ev%d" % q], 1)
            todo = [(0, full[0:8]), (1, full[8:16])]
        g.wait_ge(sem["e_ev%d" % q], 1)
        send([tr(T.yp[:, c + HB * o:c + HB * o + HB], land, [pair[o]], sem["rd%d" % (q // 2)], e) for o, e in todo])

    own = ports.index(core) if core in ports else None

    def result(k):
        q, h = 2 * k + own % 2, own // 2
        at = XW + CS * s + BL * q + HB * h
        slot = T.xg[:, at:at + HB]
        return slot, (slot if is_r else T.sm[:, HB * k:HB * k + HB])

    def collect(k):
        if own is None:
            return
        V.wait_ge(sem["rd%d" % k], 6 * 8 + 16)
        V.wait_ge(sem["e_so%d" % k], 1)
        r, f, w = 8 * HB * k, 4 * HB * k, 2 * HB * k
        v(V.tensor_tensor(T.t4[:, f:f + 4 * HB], T.red[:, r:r + 4 * HB], T.red[:, r + 4 * HB:r + 8 * HB], ADD))
        vw()
        v(V.tensor_tensor(T.t2[:, w:w + 2 * HB], T.t4[:, f:f + 2 * HB], T.t4[:, f + 2 * HB:f + 4 * HB], ADD))
        vw()
        V.tensor_tensor(result(k)[1], T.t2[:, w:w + HB], T.t2[:, w + HB:w + 2 * HB], ADD).then_inc(sem["e_red%d" % k], 1)

    def deliver(k):
        if own is None:
            return
        slot, out = result(k)
        g.wait_ge(sem["e_red%d" % k], 1)
        trs = [tr(out, slot, [T.cores[d] for d in order], sem.gg, low)]
        if not is_r:
            trs.append(tr(out, slot, [R], sem.gg, up))
        send(trs)

    if is_r:
        E.wait_ge(sem.q_w1a, 16)
    else:
        E.wait_ge(sem.w1_in, 4 if me > 3 else 32 if me == 2 else 8)
    layer1(0)
    layer1(1)
    if is_r:
        E.wait_ge(sem.q_w2a, 16)
        E.wait_ge(sem.e_fo, 1)
    else:
        E.wait_ge(sem.w2_in, 8 if me == 1 else 4)
    layer2(0)
    home(0)
    layer1(2)
    layer2(1)
    home(1)
    layer1(3)
    collect(0)
    layer2(2)
    if own is not None and own % 2 == 0:
        deliver(0)
        home(2)
    else:
        home(2)
        deliver(0)
    layer2(3)
    home(3)
    collect(1)
    deliver(1)

    if is_r:
        for q in (V, A):
            q.wait_ge(sem.gg, 2 * 15 * 8)
            q.wait_ge(sem.e_red0, 1)
            q.wait_ge(sem.e_red1, 1)
            q.wait_ge(sem.e_fo, 1)
        pieces = [(0, 512, V), (1024, 512, A), (512, 256, V), (1536, 256, A), (768, 256, V), (1792, 256, A)]
        for i, (c, n, q) in enumerate(pieces):
            src = T.xg[:].indirect(T.fo[:, c // 16:(c + n) // 16])
            out = T.yo[:, c:c + n]
            ins = V.tensor_copy(out, src) if q is V else A.activation(out, src, COPY)
            ins.then_inc(sem["fin%d" % i], 1)
        for i, (c, n, q) in enumerate(pieces):
            Y.wait_ge(sem["fin%d" % i], 1)
            Y.dma_start(T.y[:, c:c + n], T.yo[:, c:c + n]).then_inc(sem.q_y, 16)
        Y.wait_ge(sem.q_y, 16 * len(pieces))

    vw()
    if nls[0]:
        g.wait_ge(sem.ls, nls[0])
